import numpy as np, ml_dtypes
CORES = [23,119,17,113]
N = 4
TK = 64
def setup_inputs(rng):
    return {"c": rng.standard_normal((N, 128, 128), dtype=np.float32).astype(ml_dtypes.bfloat16), "x": rng.standard_normal((N, 128, TK), dtype=np.float32).astype(ml_dtypes.bfloat16)}
def setup_inputs_big(rng):
    d = setup_inputs(rng)
    for k in ("c", "x"): d[k] = (d[k].astype(np.float32) * 1024.0).astype(d[k].dtype)
    return d
def setup_inputs_small(rng):
    d = setup_inputs(rng)
    for k in ("c", "x"): d[k] = (d[k].astype(np.float32) * (1 / 1024.0)).astype(d[k].dtype)
    return d
def setup_inputs_apart(rng):
    d = setup_inputs(rng)
    f = (10.0 ** rng.permutation(np.linspace(-1.5, 1.5, N))).astype(np.float32).reshape(N, 1, 1)
    for k in ("c", "x"): d[k] = (d[k].astype(np.float32) * f).astype(d[k].dtype)
    return d
def reference(c, x):
    C, X = c.astype(np.float64), x.astype(np.float64)
    y = np.zeros((N, 128, TK))
    for r in range(N):
        for j in range(N):
            y[r] += C[(r - j) % N].T @ X[j]
    return {"y": y.astype(ml_dtypes.bfloat16 if x.dtype != np.float64 else np.float64)}

from concourse.bass import DstId, RemoteDMATransfer

N = 4
CW = 128
XW = 64
SW = CW + XW
PER = 4

SCRATCH = {
    "all": ("sbuf", [128, N * SW], "bfloat16"),
    "acc": ("psum", [128, XW], "float32"),
    "out": ("sbuf", [128, XW], "bfloat16"),
}
SEMAPHORES = ["ld", "sent", "a0", "a1", "a2", "a3", "mm", "cp", "st"]


def _bits(mask):
    return [e for e in range(mask.bit_length()) if (mask >> e) & 1]


def _plan_masks(core, peers, topo):
    allowed = {d: _bits(topo.mask(core, d)) for d in peers}
    used, plan = set(), {}
    for d in sorted(peers, key=lambda d: len(allowed[d])):
        free = [e for e in allowed[d] if e not in used]
        free.sort(key=lambda e: (sum(1 for o in peers if o not in plan and o != d and e in allowed[o]), e))
        take = free[:PER]
        assert len(take) == PER
        used.update(take)
        plan[d] = sum(1 << e for e in take)
    return plan


def rank_program(g, core, T, topo):
    rank = T.rank_of(core)
    if rank is None:
        return
    cores = list(T.cores)
    peers = [d for d in cores if d != core]

    def slot(q):
        return T.all[:, q * SW:(q + 1) * SW]

    def c_of(q):
        return T.all[:, q * SW:q * SW + CW]

    def x_of(q):
        return T.all[:, q * SW + CW:(q + 1) * SW]

    g.sync.dma_start(c_of(rank), T.c[:, :]).then_inc(T.sem.ld, 16)
    g.scalar.dma_start(x_of(rank), T.x[:, :]).then_inc(T.sem.ld, 16)

    plan = _plan_masks(core, peers, topo)
    transfers = []
    for d in peers:
        assert topo.may_write(core, d)
        rid, pid, _ = topo.addr(d)
        transfers.append(RemoteDMATransfer(dst_ids=[DstId(rid=rid, pnc=pid)], dma_engine_mask=plan[d],
                                           remote_sem=T.sem["a%d" % rank], src=slot(rank), dst=slot(rank)))
    g.wait_ge(T.sem.ld, 32)
    g.remote_dma_fused(transfers, local_sem=T.sem.sent)

    def when(q):
        s = cores[q]
        if s == core:
            return 0
        if topo.chip(s) == topo.chip(core):
            return 1
        return 2 if topo.die(s) == topo.die(core) else 3

    terms = sorted(range(N), key=lambda j: (max(when((rank - j) % N), when(j)), j))
    waited = set()
    for i, j in enumerate(terms):
        k = (rank - j) % N
        for q in sorted({k, j}, key=when):
            if q not in waited:
                waited.add(q)
                if q == rank:
                    g.tensor.wait_ge(T.sem.ld, 32)
                else:
                    g.tensor.wait_ge(T.sem["a%d" % q], PER)
        mm = g.tensor.matmul(T.acc[:, :], c_of(k), x_of(j), i == 0, i == N - 1)
    mm.then_inc(T.sem.mm, 1)

    g.vector.wait_ge(T.sem.mm, 1)
    g.vector.tensor_copy(T.out[:, :], T.acc[:, :]).then_inc(T.sem.cp, 1)
    g.sync.wait_ge(T.sem.cp, 1)
    g.sync.dma_start(T.y[:, :], T.out[:, :]).then_inc(T.sem.st, 16)
    g.wait_ge(T.sem.sent, PER * len(peers))
    g.sync.wait_ge(T.sem.st, 16)
